import numpy as np
import ml_dtypes


def mxq(x, axis, fmt="e4m3"):
    dtype, down = {"e4m3": (ml_dtypes.float8_e4m3fn, 7), "e5m2": (ml_dtypes.float8_e5m2, 14)}[fmt]
    v = np.moveaxis(np.asarray(x, np.float32).astype(ml_dtypes.bfloat16).astype(np.float64), axis, -1)
    blocks = v.reshape(v.shape[:-1] + (-1, 32))
    amax = np.abs(blocks).max(-1, keepdims=True)
    byte = np.maximum(np.where(amax > 0, np.frexp(amax)[1] - 1 + 127, 0) - down, 1)
    scale = np.exp2(byte - 127.0)
    codes = (blocks / scale).astype(np.float32).astype(dtype).astype(np.float64)
    return np.moveaxis((codes * scale).reshape(v.shape), -1, axis)


WIDE = False


def mx_kscale(k):
    if not WIDE:
        return np.ones(k)
    levels = np.array([10, -10, 5, -5, 0])
    if k % 512:
        return np.exp2(np.random.permutation(np.resize(levels, k // 32))).repeat(32)
    a = np.empty((k // 512, 16))
    for p in range(k // 512):
        a[p, :8] = np.random.permutation(np.resize(levels, 8))
        for g in range(8):
            far = levels[np.abs(levels - a[p, g]) >= 10]
            a[p, g + 8] = far[np.random.randint(len(far))]
    return np.exp2(a.ravel()).repeat(32)


def f64(x):
    return np.asarray(x).astype(np.float64)


def striped(idx):
    return np.tile(idx.reshape(-1, 16).T, (8, 1)).astype(np.uint16)


def unstriped(offs):
    return offs[:16].T.reshape(-1).astype(np.int64)


def striped8(idx):
    return np.concatenate([x.reshape(-1, 16).T for x in idx]).astype(np.uint16)


def runs(offs, k):
    lists = np.stack([offs[16 * r : 16 * r + 16].T.reshape(-1) for r in range(8)]).astype(np.int64)
    return lists[np.arange(k) % 512 // 64]


def pack_weight(w):
    k, n = w.shape
    w = f64(np.asarray(w, np.float32).astype(ml_dtypes.bfloat16)).reshape(k // 32, 32, n)
    amax = np.abs(w).max(1)
    byte = np.clip(np.where(amax > 0, np.frexp(amax)[1] - 1 + 127 - 7, 1), 1, 254)
    scaled = (w * np.exp2(127.0 - byte)[:, None, :]).reshape(k, n).astype(np.float32)
    words = np.ascontiguousarray(scaled.reshape(k // 512, 128, 4, n).transpose(0, 1, 3, 2)).astype(ml_dtypes.float8_e4m3fn).view(np.uint8)
    return words, np.ascontiguousarray(byte.astype(np.uint8).reshape(k // 512, 16, n))


def unpack_weight(words, scales):
    g, p, n, _ = words.shape
    vals = np.ascontiguousarray(words).view(ml_dtypes.float8_e4m3fn).astype(np.float64) * np.repeat(np.exp2(scales.astype(np.float64) - 127.0), 8, axis=1)[..., None]
    return vals.transpose(0, 1, 3, 2).reshape(g * 512, n)


def sigmoid(v):
    return 1.0 / (1.0 + np.exp(-np.maximum(v, -700.0)))


K, T, S, N, H, W = 512, 2048, 512, 512, 512, 256


def setup_inputs():
    n = np.random.standard_normal
    s = mx_kscale(K)[:, None]
    u = mx_kscale(H)
    packed_xT = pack_weight(n((K, T)) * s)
    perm = np.stack([np.random.permutation(S) for _ in range(8)])
    return {
        "x_words": packed_xT[0],
        "x_scales": packed_xT[1],
        "w1": (n((K, H)) / np.sqrt(K) / s).astype(np.float32),
        "gn": (np.random.uniform(0.5, 1.5, (H, 1)) * u[:, None]).astype(np.float32),
        "w2": (n((H, N)) / np.sqrt(H) / u[:, None]).astype(np.float32),
        "offs": striped(np.random.permutation(T)[:S]),
        "n1": striped8(perm[:, :W]),
        "n2": striped8(perm[:, W:]),
        "n3": striped8(np.stack([np.random.permutation(S) for _ in range(8)])),
        "n4": striped8(np.stack([np.random.permutation(S) for _ in range(8)])),
    }


def reference(x_words, x_scales, w1, gn, w2, offs, n1, n2, n3, n4):
    xq = unpack_weight(x_words, x_scales)[:, unstriped(offs)]
    y = mxq(f64(w1), 0, "e4m3").T @ xq
    pa = y[np.arange(H)[:, None], runs(n1, H)]
    pb = y[np.arange(H)[:, None], runs(n2, H)]
    ra = pa * sigmoid(pb)
    ds = y.copy()
    ds[np.arange(H)[:, None], runs(n2, H)] = ra
    z = f64(gn) * ds
    h = mxq(f64(w2), 0, "e4m3").T @ mxq(z, 0, "e4m3")
    sm = np.maximum(h, h[np.arange(N)[:, None], runs(n4, N)])
    ds2 = np.zeros((N, S))
    ds2[np.arange(N)[:, None], runs(n3, N)] = sm
    return ds2 * sigmoid(h)

@@ -1,0 +1,174 @@
+from contextlib import ExitStack
+
+import concourse.mybir as mybir
+
+K, T, S, H, N, W = 512, 2048, 512, 512, 512, 256
+FLOPS = 2 * K * H * S + 2 * H * N * S
+
+F32 = mybir.dt.float32
+BF16 = mybir.dt.bfloat16
+I32 = mybir.dt.int32
+U32 = mybir.dt.uint32
+U16 = mybir.dt.uint16
+U8 = mybir.dt.uint8
+FP8X4 = mybir.dt.float8_e4m3fn_x4
+ACT = mybir.ActivationFunctionType
+ALU = mybir.AluOpType
+
+P = 128
+PACK = 4
+HALF = S // 2
+LIST_COLS = 16
+
+
+def tile_picked_layfoldsendg_none_p_kernel(tc, x_words, x_scales, w1, gn, w2, offs, n1, n2, n3, n4, out):
+    nc = tc.nc
+    halves = [slice(0, HALF), slice(HALF, S)]
+    half_lists = [slice(0, HALF // LIST_COLS), slice(HALF // LIST_COLS, S // LIST_COLS)]
+
+    with ExitStack() as ctx:
+        keep = ctx.enter_context(tc.tile_pool(name="keep", bufs=1))
+        psum = ctx.enter_context(tc.psum_pool(name="psum", bufs=1))
+
+        def sb(shape, dtype, name, tag=None):
+            return keep.tile(shape, dtype, name=name, tag=tag or name, align_bytes=64)
+
+        xs_all = sb([P, T], U8, "xs_all")
+        nc.gpsimd.memset(xs_all[:].bitcast(I32), 0)
+        warm_in = sb([P, 1], F32, "warm_in")
+        warm_out = sb([P, 1], F32, "warm_out")
+        nc.vector.memset(warm_in[:], 0.0)
+
+        w1_raw = sb([P, PACK, H], F32, "w1_raw")
+        nc.sync.dma_start(out=w1_raw[:], in_=w1.rearrange("(p j) c -> p j c", j=PACK))
+        offs_sb = sb([P, S // LIST_COLS], U16, "offs_sb")
+        nc.sync.dma_start(offs_sb[:], offs)
+        for q in range(4):
+            nc.sync.dma_start(out=xs_all[32 * q : 32 * q + 4, :].bitcast(I32), in_=x_scales[0, 4 * q : 4 * q + 4, :].bitcast(I32))
+        nc.scalar.activation(warm_out[:], warm_in[:], ACT.Sigmoid)
+        xw_all = sb([P, T], U32, "xw_all")
+        nc.sync.dma_start(out=xw_all[:].bitcast(I32), in_=x_words[0].rearrange("p c r -> p (c r)").bitcast(I32))
+        n1_sb = sb([P, W // LIST_COLS], U16, "n1_sb")
+        nc.sync.dma_start(n1_sb[:], n1)
+        n2_sb = sb([P, W // LIST_COLS], U16, "n2_sb")
+        nc.sync.dma_start(n2_sb[:], n2)
+        w2_raw = sb([P, PACK, N], F32, "w2_raw")
+        nc.sync.dma_start(out=w2_raw[:], in_=w2.rearrange("(p j) c -> p j c", j=PACK))
+        gain = sb([P, PACK], F32, "gain")
+        nc.sync.dma_start(out=gain[:], in_=gn.rearrange("(p t) o -> p (t o)", t=PACK))
+        n4_sb = sb([P, S // LIST_COLS], U16, "n4_sb")
+        nc.sync.dma_start(n4_sb[:], n4)
+        n3_sb = sb([P, S // LIST_COLS], U16, "n3_sb")
+        nc.sync.dma_start(n3_sb[:], n3)
+
+        def deal(copy, grouped, raw, ms, ts):
+            copy(
+                grouped[:].rearrange("p (t m j) -> p m j t", m=P, j=PACK)[:, ms],
+                raw[:].rearrange("p j (m t) -> p m j t", t=PACK)[:, ms, :, ts],
+            )
+
+        def quantize(values, width, name):
+            codes = sb([P, width], U32, name + "_codes")
+            scales = sb([P, width], U8, name + "_scales")
+            nc.vector.quantize_mx(out=codes[:].bitcast(FP8X4), scales=scales[:], in_=values)
+            return codes, scales
+
+        def product(acc, t, w_mx, x_codes, x_scale):
+            nc.tensor.matmul_mx(
+                out=acc,
+                lhsT=w_mx[0][:, t * P : (t + 1) * P].bitcast(FP8X4),
+                lhsT_scale=w_mx[1][:, t * P : (t + 1) * P],
+                rhs=x_codes.bitcast(FP8X4),
+                rhs_scale=x_scale,
+                start=True,
+                stop=True,
+            )
+
+        def banks(t):
+            parts = halves if t == 0 else [slice(0, S)]
+            return [(psum.tile([P, cols.stop - cols.start], F32, name="acc", tag="bank%d_%d" % (t, c)), cols) for c, cols in enumerate(parts)]
+
+        xs = sb([P, S], U8, "xs")
+        nc.vector.tensor_copy(xs[:], xs_all[:].indirect(offs_sb[:]))
+        w1_bf = sb([P, PACK * H], BF16, "w1_bf")
+        deal(nc.scalar.copy, w1_bf, w1_raw, slice(96, P), slice(0, PACK))
+        deal(nc.vector.tensor_copy, w1_bf, w1_raw, slice(0, 96), slice(0, PACK))
+        w1_mx = quantize(w1_bf[:], H, "w1")
+        xw = sb([P, S], U32, "xw")
+        for cols, lists in zip(halves, half_lists):
+            nc.vector.tensor_copy(xw[:, cols], xw_all[:].indirect(offs_sb[:, lists]))
+
+        ys, gates = [], []
+        for t in range(PACK):
+            y = sb([P, S], F32, "y%d" % t)
+            for acc, cols in banks(t):
+                product(acc[:], t, w1_mx, xw[:, cols], xs[:, cols])
+                nc.scalar.copy(y[:, cols], acc[:])
+            gate = sb([P, W], F32, "gate%d" % t)
+            nc.scalar.activation(gate[:], y[:].indirect(n2_sb[:]), ACT.Sigmoid)
+            ys.append(y)
+            gates.append(gate)
+        for t in range(PACK):
+            pa = sb([P, W], F32, "pa%d" % t)
+            nc.vector.tensor_copy(pa[:], ys[t][:].indirect(n1_sb[:]))
+            nc.vector.tensor_tensor(ys[t][:].indirect(n2_sb[:]), pa[:], gates[t][:], ALU.mult)
+        pairs = [sb([P, 2, HALF, 2], BF16, "pairs%d" % c) for c in range(2)]
+        w2_mx = []
+        for t in range(PACK):
+            for c, cols in enumerate(halves):
+                nc.scalar.activation(pairs[c][:, t // 2, :, t % 2], ys[t][:, cols], ACT.Copy, scale=gain[:, t : t + 1])
+            if t == 0:
+                w2_bf = sb([P, 2 * N], BF16, "w2_bf0")
+                deal(nc.scalar.copy, w2_bf, w2_raw, slice(0, P), slice(0, 2))
+                w2_mx.append(quantize(w2_bf[:], N // 2, "w2_0"))
+
+        z_mx = []
+        for c in range(2):
+            z = sb([P, HALF * PACK], BF16, "z%d" % c)
+            nc.vector.tensor_copy(
+                z[:].bitcast(F32).rearrange("p (s u) -> p s u", u=2),
+                pairs[c][:].rearrange("p u s e -> p u (s e)").bitcast(F32).rearrange("p u s -> p s u"),
+            )
+            z_mx.append(quantize(z[:], HALF, "z%d" % c))
+        w2_bf = sb([P, 2 * N], BF16, "w2_bf1", tag="z1")
+        deal(nc.vector.tensor_copy, w2_bf, w2_raw, slice(0, P), slice(2, 4))
+        w2_mx.append(quantize(w2_bf[:], N // 2, "w2_1"))
+
+        out_rows = out.rearrange("(p t) s -> p t s", t=PACK)
+        hs, diffs, sents, out_gates = {}, {}, {}, {}
+
+        def fetch(t):
+            h = sb([P, S], F32, "h%d" % t)
+            h_again = sb([P, S], F32, "h_again%d" % t)
+            for acc, cols in banks(t):
+                for c in range(2):
+                    if cols.start <= c * HALF < cols.stop:
+                        product(acc[:, c * HALF - cols.start : (c + 1) * HALF - cols.start], t % 2, w2_mx[t // 2], z_mx[c][0][:], z_mx[c][1][:])
+                nc.scalar.copy(h[:, cols], acc[:])
+                nc.scalar.copy(h_again[:, cols], acc[:])
+            diff = sb([P, S], F32, "diff%d" % t)
+            for cols, lists in zip(halves, half_lists):
+                nc.vector.tensor_tensor(diff[:, cols], h[:].indirect(n4_sb[:, lists]), h_again[:, cols], ALU.subtract)
+            hs[t], diffs[t] = h, diff
+
+        def send(t):
+            excess = sb([P, S], F32, "excess%d" % t)
+            nc.scalar.activation(excess[:], diffs[t][:], ACT.Relu)
+            sents[t] = sb([P, 2 * S], F32, "sent%d" % t)
+            nc.vector.tensor_tensor(sents[t][:].indirect(n3_sb[:]), excess[:], hs[t][:], ALU.add)
+
+        def finish(t):
+            gate = sb([P, S], F32, "out_gate%d" % t)
+            nc.scalar.activation(gate[:], hs[t][:], ACT.Sigmoid)
+            result = sb([P, S], F32, "result%d" % t)
+            for c, cols in enumerate(halves if t == PACK - 1 else [slice(0, S)]):
+                nc.vector.tensor_tensor(result[:, cols], sents[t][:, cols], gate[:, cols], ALU.mult)
+                (nc.sync, nc.scalar)[c].dma_start(out=out_rows[:, t, cols], in_=result[:, cols])
+
+        for step in range(PACK + 2):
+            if step < PACK:
+                fetch(step)
+            if 1 <= step <= PACK:
+                send(step - 1)
+            if step >= 2:
+                finish(step - 2)

@@ -139,36 +139,37 @@ def tile_picked_layfoldsendg_none_p_kernel(tc, x_words, x_scales, w1, gn, w2, of
 
         def fetch(t):
             h = sb([P, S], F32, "h%d" % t)
-            h_again = sb([P, S], F32, "h_again%d" % t)
             for acc, cols in banks(t):
                 for c in range(2):
                     if cols.start <= c * HALF < cols.stop:
                         product(acc[:, c * HALF - cols.start : (c + 1) * HALF - cols.start], t % 2, w2_mx[t // 2], z_mx[c][0][:], z_mx[c][1][:])
                 nc.scalar.copy(h[:, cols], acc[:])
-                nc.scalar.copy(h_again[:, cols], acc[:])
-            diff = sb([P, S], F32, "diff%d" % t)
+            other = sb([P, S], F32, "other%d" % t)
             for cols, lists in zip(halves, half_lists):
-                nc.vector.tensor_tensor(diff[:, cols], h[:].indirect(n4_sb[:, lists]), h_again[:, cols], ALU.subtract)
-            hs[t], diffs[t] = h, diff
+                nc.vector.tensor_copy(other[:, cols], h[:].indirect(n4_sb[:, lists]))
+            hs[t], diffs[t] = h, other
 
         def send(t):
-            excess = sb([P, S], F32, "excess%d" % t)
-            nc.scalar.activation(excess[:], diffs[t][:], ACT.Relu)
+            diff = sb([P, S], F32, "diff%d" % t, tag=(None, "z1_codes", "excess1", "excess2")[t])
+            excess = sb([P, S], F32, "excess%d" % t, tag="z1_codes" if t == 0 else None)
+            larger = sb([P, S], F32, "larger%d" % t)
+            for cols in halves:
+                nc.gpsimd.tensor_tensor(diff[:, cols], diffs[t][:, cols], hs[t][:, cols], ALU.subtract)
+                nc.scalar.activation(excess[:, cols], diff[:, cols], ACT.Relu)
+            for cols in halves:
+                nc.gpsimd.tensor_tensor(larger[:, cols], excess[:, cols], hs[t][:, cols], ALU.add)
             sents[t] = sb([P, 2 * S], F32, "sent%d" % t)
-            nc.vector.tensor_tensor(sents[t][:].indirect(n3_sb[:]), excess[:], hs[t][:], ALU.add)
+            nc.vector.tensor_copy(sents[t][:].indirect(n3_sb[:]), larger[:])
 
         def finish(t):
             gate = sb([P, S], F32, "out_gate%d" % t)
             nc.scalar.activation(gate[:], hs[t][:], ACT.Sigmoid)
-            result = sb([P, S], F32, "result%d" % t)
-            for c, cols in enumerate(halves if t == PACK - 1 else [slice(0, S)]):
-                nc.vector.tensor_tensor(result[:, cols], sents[t][:, cols], gate[:, cols], ALU.mult)
-                (nc.sync, nc.scalar)[c].dma_start(out=out_rows[:, t, cols], in_=result[:, cols])
+            result = sb([P, S], F32, "result%d" % t, tag=("excess3", "out_gate0", "out_gate1", None)[t])
+            last = t == PACK - 1
+            for cols in halves if last else [slice(0, S)]:
+                (nc.vector if last else nc.gpsimd).tensor_tensor(result[:, cols], sents[t][:, cols], gate[:, cols], ALU.mult)
+                (nc.scalar if last else nc.sync).dma_start(out=out_rows[:, t, cols], in_=result[:, cols])
 
-        for step in range(PACK + 2):
-            if step < PACK:
-                fetch(step)
-            if 1 <= step <= PACK:
-                send(step - 1)
-            if step >= 2:
-                finish(step - 2)
+        for stage in (fetch, send, finish):
+            for t in range(PACK):
+                stage(t)

@@ -19,11 +19,13 @@ P = 128
 PACK = 4
 HALF = S // 2
 LIST_COLS = 16
+EARLY = 32
 
 
 def tile_picked_layfoldsendg_none_p_kernel(tc, x_words, x_scales, w1, gn, w2, offs, n1, n2, n3, n4, out):
     nc = tc.nc
     halves = [slice(0, HALF), slice(HALF, S)]
+    pieces = [slice(0, 128), slice(128, 384), slice(384, S)]
     half_lists = [slice(0, HALF // LIST_COLS), slice(HALF // LIST_COLS, S // LIST_COLS)]
 
     with ExitStack() as ctx:
@@ -67,8 +69,8 @@ def tile_picked_layfoldsendg_none_p_kernel(tc, x_words, x_scales, w1, gn, w2, of
                 raw[:].rearrange("p j (m t) -> p m j t", t=PACK)[:, ms, :, ts],
             )
 
-        def quantize(values, width, name):
-            codes = sb([P, width], U32, name + "_codes")
+        def quantize(values, width, name, tag=None):
+            codes = sb([P, width], U32, name + "_codes", tag=tag)
             scales = sb([P, width], U8, name + "_scales")
             nc.vector.quantize_mx(out=codes[:].bitcast(FP8X4), scales=scales[:], in_=values)
             return codes, scales
@@ -84,16 +86,17 @@ def tile_picked_layfoldsendg_none_p_kernel(tc, x_words, x_scales, w1, gn, w2, of
                 stop=True,
             )
 
-        def banks(t):
-            parts = halves if t == 0 else [slice(0, S)]
+        def banks(t, first_parts):
+            parts = first_parts if t == 0 else [slice(0, S)]
             return [(psum.tile([P, cols.stop - cols.start], F32, name="acc", tag="bank%d_%d" % (t, c)), cols) for c, cols in enumerate(parts)]
 
         xs = sb([P, S], U8, "xs")
         nc.vector.tensor_copy(xs[:], xs_all[:].indirect(offs_sb[:]))
-        w1_bf = sb([P, PACK * H], BF16, "w1_bf")
-        deal(nc.scalar.copy, w1_bf, w1_raw, slice(96, P), slice(0, PACK))
-        deal(nc.vector.tensor_copy, w1_bf, w1_raw, slice(0, 96), slice(0, PACK))
-        w1_mx = quantize(w1_bf[:], H, "w1")
+        w1_mx = []
+        for u, copy in enumerate((nc.vector.tensor_copy, nc.scalar.copy)):
+            w1_bf = sb([P, 2 * H], BF16, "w1_bf%d" % u)
+            deal(copy, w1_bf, w1_raw, slice(0, P), slice(2 * u, 2 * u + 2))
+            w1_mx.append(quantize(w1_bf[:], H // 2, "w1_%d" % u))
         xw = sb([P, S], U32, "xw")
         for cols, lists in zip(halves, half_lists):
             nc.vector.tensor_copy(xw[:, cols], xw_all[:].indirect(offs_sb[:, lists]))
@@ -101,8 +104,8 @@ def tile_picked_layfoldsendg_none_p_kernel(tc, x_words, x_scales, w1, gn, w2, of
         ys, gates = [], []
         for t in range(PACK):
             y = sb([P, S], F32, "y%d" % t)
-            for acc, cols in banks(t):
-                product(acc[:], t, w1_mx, xw[:, cols], xs[:, cols])
+            for acc, cols in banks(t, halves):
+                product(acc[:], t % 2, w1_mx[t // 2], xw[:, cols], xs[:, cols])
                 nc.scalar.copy(y[:, cols], acc[:])
             gate = sb([P, W], F32, "gate%d" % t)
             nc.scalar.activation(gate[:], y[:].indirect(n2_sb[:]), ACT.Sigmoid)
@@ -112,37 +115,39 @@ def tile_picked_layfoldsendg_none_p_kernel(tc, x_words, x_scales, w1, gn, w2, of
             pa = sb([P, W], F32, "pa%d" % t)
             nc.vector.tensor_copy(pa[:], ys[t][:].indirect(n1_sb[:]))
             nc.vector.tensor_tensor(ys[t][:].indirect(n2_sb[:]), pa[:], gates[t][:], ALU.mult)
-        pairs = [sb([P, 2, HALF, 2], BF16, "pairs%d" % c) for c in range(2)]
+        pairs = [sb([P, 2, cols.stop - cols.start, 2], BF16, "pairs%d" % c) for c, cols in enumerate(pieces)]
         w2_mx = []
         for t in range(PACK):
-            for c, cols in enumerate(halves):
+            for c, cols in enumerate(pieces):
                 nc.scalar.activation(pairs[c][:, t // 2, :, t % 2], ys[t][:, cols], ACT.Copy, scale=gain[:, t : t + 1])
             if t == 0:
                 w2_bf = sb([P, 2 * N], BF16, "w2_bf0")
                 deal(nc.scalar.copy, w2_bf, w2_raw, slice(0, P), slice(0, 2))
                 w2_mx.append(quantize(w2_bf[:], N // 2, "w2_0"))
+                w2_late = sb([P, 2 * N], BF16, "w2_bf1")
+                deal(nc.scalar.copy, w2_late, w2_raw, slice(0, EARLY), slice(2, 4))
+
+        deal(nc.scalar.copy, w2_late, w2_raw, slice(EARLY, P), slice(2, 4))
 
         z_mx = []
-        for c in range(2):
-            z = sb([P, HALF * PACK], BF16, "z%d" % c)
+        for c, cols in enumerate(pieces):
+            z = sb([P, (cols.stop - cols.start) * PACK], BF16, "z%d" % c)
             nc.vector.tensor_copy(
                 z[:].bitcast(F32).rearrange("p (s u) -> p s u", u=2),
                 pairs[c][:].rearrange("p u s e -> p u (s e)").bitcast(F32).rearrange("p u s -> p s u"),
             )
-            z_mx.append(quantize(z[:], HALF, "z%d" % c))
-        w2_bf = sb([P, 2 * N], BF16, "w2_bf1", tag="z1")
-        deal(nc.vector.tensor_copy, w2_bf, w2_raw, slice(0, P), slice(2, 4))
-        w2_mx.append(quantize(w2_bf[:], N // 2, "w2_1"))
+            z_mx.append(quantize(z[:], cols.stop - cols.start, "z%d" % c))
+        w2_mx.append(quantize(w2_late[:], N // 2, "w2_1", tag="z2"))
 
         out_rows = out.rearrange("(p t) s -> p t s", t=PACK)
         hs, diffs, sents, out_gates = {}, {}, {}, {}
 
         def fetch(t):
             h = sb([P, S], F32, "h%d" % t)
-            for acc, cols in banks(t):
-                for c in range(2):
-                    if cols.start <= c * HALF < cols.stop:
-                        product(acc[:, c * HALF - cols.start : (c + 1) * HALF - cols.start], t % 2, w2_mx[t // 2], z_mx[c][0][:], z_mx[c][1][:])
+            for acc, cols in banks(t, pieces):
+                for c, piece in enumerate(pieces):
+                    if cols.start <= piece.start < cols.stop:
+                        product(acc[:, piece.start - cols.start : piece.stop - cols.start], t % 2, w2_mx[t // 2], z_mx[c][0][:], z_mx[c][1][:])
                 nc.scalar.copy(h[:, cols], acc[:])
             other = sb([P, S], F32, "other%d" % t)
             for cols, lists in zip(halves, half_lists):
@@ -150,8 +155,8 @@ def tile_picked_layfoldsendg_none_p_kernel(tc, x_words, x_scales, w1, gn, w2, of
             hs[t], diffs[t] = h, other
 
         def send(t):
-            diff = sb([P, S], F32, "diff%d" % t, tag=(None, "z1_codes", "excess1", "excess2")[t])
-            excess = sb([P, S], F32, "excess%d" % t, tag="z1_codes" if t == 0 else None)
+            diff = sb([P, S], F32, "diff%d" % t, tag="excess%d" % (t - 1) if t else None)
+            excess = sb([P, S], F32, "excess%d" % t)
             larger = sb([P, S], F32, "larger%d" % t)
             for cols in halves:
                 nc.gpsimd.tensor_tensor(diff[:, cols], diffs[t][:, cols], hs[t][:, cols], ALU.subtract)

from contextlib import ExitStack

import concourse.mybir as mybir

K, T, S, H, N, W = 512, 2048, 512, 512, 512, 256
FLOPS = 2 * K * H * S + 2 * H * N * S

F32 = mybir.dt.float32
BF16 = mybir.dt.bfloat16
I32 = mybir.dt.int32
U32 = mybir.dt.uint32
U16 = mybir.dt.uint16
U8 = mybir.dt.uint8
FP8X4 = mybir.dt.float8_e4m3fn_x4
ACT = mybir.ActivationFunctionType
ALU = mybir.AluOpType

P = 128
PACK = 4
HALF = S // 2
LIST_COLS = 16
EARLY = 32


def tile_picked_layfoldsendg_none_p_kernel(tc, x_words, x_scales, w1, gn, w2, offs, n1, n2, n3, n4, out):
    nc = tc.nc
    halves = [slice(0, HALF), slice(HALF, S)]
    pieces = [slice(0, 128), slice(128, 384), slice(384, S)]
    half_lists = [slice(0, HALF // LIST_COLS), slice(HALF // LIST_COLS, S // LIST_COLS)]

    with ExitStack() as ctx:
        keep = ctx.enter_context(tc.tile_pool(name="keep", bufs=1))
        psum = ctx.enter_context(tc.psum_pool(name="psum", bufs=1))

        def sb(shape, dtype, name, tag=None):
            return keep.tile(shape, dtype, name=name, tag=tag or name, align_bytes=64)

        xs_all = sb([P, T], U8, "xs_all")
        nc.gpsimd.memset(xs_all[:].bitcast(I32), 0)
        warm_in = sb([P, 1], F32, "warm_in")
        warm_out = sb([P, 1], F32, "warm_out")
        nc.vector.memset(warm_in[:], 0.0)

        w1_raw = sb([P, PACK, H], F32, "w1_raw")
        nc.sync.dma_start(out=w1_raw[:], in_=w1.rearrange("(p j) c -> p j c", j=PACK))
        offs_sb = sb([P, S // LIST_COLS], U16, "offs_sb")
        nc.sync.dma_start(offs_sb[:], offs)
        for q in range(4):
            nc.sync.dma_start(out=xs_all[32 * q : 32 * q + 4, :].bitcast(I32), in_=x_scales[0, 4 * q : 4 * q + 4, :].bitcast(I32))
        nc.scalar.activation(warm_out[:], warm_in[:], ACT.Sigmoid)
        xw_all = sb([P, T], U32, "xw_all")
        nc.sync.dma_start(out=xw_all[:].bitcast(I32), in_=x_words[0].rearrange("p c r -> p (c r)").bitcast(I32))
        n1_sb = sb([P, W // LIST_COLS], U16, "n1_sb")
        nc.sync.dma_start(n1_sb[:], n1)
        n2_sb = sb([P, W // LIST_COLS], U16, "n2_sb")
        nc.sync.dma_start(n2_sb[:], n2)
        w2_raw = sb([P, PACK, N], F32, "w2_raw")
        nc.sync.dma_start(out=w2_raw[:], in_=w2.rearrange("(p j) c -> p j c", j=PACK))
        gain = sb([P, PACK], F32, "gain")
        nc.sync.dma_start(out=gain[:], in_=gn.rearrange("(p t) o -> p (t o)", t=PACK))
        n4_sb = sb([P, S // LIST_COLS], U16, "n4_sb")
        nc.sync.dma_start(n4_sb[:], n4)
        n3_sb = sb([P, S // LIST_COLS], U16, "n3_sb")
        nc.sync.dma_start(n3_sb[:], n3)

        def deal(copy, grouped, raw, ms, ts):
            copy(
                grouped[:].rearrange("p (t m j) -> p m j t", m=P, j=PACK)[:, ms],
                raw[:].rearrange("p j (m t) -> p m j t", t=PACK)[:, ms, :, ts],
            )

        def quantize(values, width, name, tag=None):
            codes = sb([P, width], U32, name + "_codes", tag=tag)
            scales = sb([P, width], U8, name + "_scales")
            nc.vector.quantize_mx(out=codes[:].bitcast(FP8X4), scales=scales[:], in_=values)
            return codes, scales

        def product(acc, t, w_mx, x_codes, x_scale):
            nc.tensor.matmul_mx(
                out=acc,
                lhsT=w_mx[0][:, t * P : (t + 1) * P].bitcast(FP8X4),
                lhsT_scale=w_mx[1][:, t * P : (t + 1) * P],
                rhs=x_codes.bitcast(FP8X4),
                rhs_scale=x_scale,
                start=True,
                stop=True,
            )

        def banks(t, first_parts):
            parts = first_parts if t == 0 else [slice(0, S)]
            return [(psum.tile([P, cols.stop - cols.start], F32, name="acc", tag="bank%d_%d" % (t, c)), cols) for c, cols in enumerate(parts)]

        xs = sb([P, S], U8, "xs")
        nc.vector.tensor_copy(xs[:], xs_all[:].indirect(offs_sb[:]))
        w1_mx = []
        for u, copy in enumerate((nc.vector.tensor_copy, nc.scalar.copy)):
            w1_bf = sb([P, 2 * H], BF16, "w1_bf%d" % u)
            deal(copy, w1_bf, w1_raw, slice(0, P), slice(2 * u, 2 * u + 2))
            w1_mx.append(quantize(w1_bf[:], H // 2, "w1_%d" % u))
        xw = sb([P, S], U32, "xw")
        for cols, lists in zip(halves, half_lists):
            nc.vector.tensor_copy(xw[:, cols], xw_all[:].indirect(offs_sb[:, lists]))

        ys, gates = [], []
        for t in range(PACK):
            y = sb([P, S], F32, "y%d" % t)
            for acc, cols in banks(t, halves):
                product(acc[:], t % 2, w1_mx[t // 2], xw[:, cols], xs[:, cols])
                nc.scalar.copy(y[:, cols], acc[:])
            gate = sb([P, W], F32, "gate%d" % t)
            nc.scalar.activation(gate[:], y[:].indirect(n2_sb[:]), ACT.Sigmoid)
            ys.append(y)
            gates.append(gate)
        for t in range(PACK):
            pa = sb([P, W], F32, "pa%d" % t)
            nc.vector.tensor_copy(pa[:], ys[t][:].indirect(n1_sb[:]))
            nc.vector.tensor_tensor(ys[t][:].indirect(n2_sb[:]), pa[:], gates[t][:], ALU.mult)
        pairs = [sb([P, 2, cols.stop - cols.start, 2], BF16, "pairs%d" % c) for c, cols in enumerate(pieces)]
        w2_mx = []
        for t in range(PACK):
            for c, cols in enumerate(pieces):
                nc.scalar.activation(pairs[c][:, t // 2, :, t % 2], ys[t][:, cols], ACT.Copy, scale=gain[:, t : t + 1])
            if t == 0:
                w2_bf = sb([P, 2 * N], BF16, "w2_bf0")
                deal(nc.scalar.copy, w2_bf, w2_raw, slice(0, P), slice(0, 2))
                w2_mx.append(quantize(w2_bf[:], N // 2, "w2_0"))
                w2_late = sb([P, 2 * N], BF16, "w2_bf1")
                deal(nc.scalar.copy, w2_late, w2_raw, slice(0, EARLY), slice(2, 4))

        deal(nc.scalar.copy, w2_late, w2_raw, slice(EARLY, P), slice(2, 4))

        z_mx = []
        for c, cols in enumerate(pieces):
            z = sb([P, (cols.stop - cols.start) * PACK], BF16, "z%d" % c)
            nc.vector.tensor_copy(
                z[:].bitcast(F32).rearrange("p (s u) -> p s u", u=2),
                pairs[c][:].rearrange("p u s e -> p u (s e)").bitcast(F32).rearrange("p u s -> p s u"),
            )
            z_mx.append(quantize(z[:], cols.stop - cols.start, "z%d" % c))
        w2_mx.append(quantize(w2_late[:], N // 2, "w2_1", tag="z2"))

        out_rows = out.rearrange("(p t) s -> p t s", t=PACK)
        hs, diffs, sents, out_gates = {}, {}, {}, {}

        def fetch(t):
            h = sb([P, S], F32, "h%d" % t)
            for acc, cols in banks(t, pieces):
                for c, piece in enumerate(pieces):
                    if cols.start <= piece.start < cols.stop:
                        product(acc[:, piece.start - cols.start : piece.stop - cols.start], t % 2, w2_mx[t // 2], z_mx[c][0][:], z_mx[c][1][:])
                nc.scalar.copy(h[:, cols], acc[:])
            other = sb([P, S], F32, "other%d" % t)
            for cols, lists in zip(halves, half_lists):
                nc.vector.tensor_copy(other[:, cols], h[:].indirect(n4_sb[:, lists]))
            hs[t], diffs[t] = h, other

        def send(t):
            diff = sb([P, S], F32, "diff%d" % t, tag="excess%d" % (t - 1) if t else None)
            excess = sb([P, S], F32, "excess%d" % t)
            larger = sb([P, S], F32, "larger%d" % t)
            for cols in halves:
                nc.gpsimd.tensor_tensor(diff[:, cols], diffs[t][:, cols], hs[t][:, cols], ALU.subtract)
                nc.scalar.activation(excess[:, cols], diff[:, cols], ACT.Relu)
            for cols in halves:
                nc.gpsimd.tensor_tensor(larger[:, cols], excess[:, cols], hs[t][:, cols], ALU.add)
            sents[t] = sb([P, 2 * S], F32, "sent%d" % t)
            nc.vector.tensor_copy(sents[t][:].indirect(n3_sb[:]), larger[:])

        def finish(t):
            gate = sb([P, S], F32, "out_gate%d" % t)
            nc.scalar.activation(gate[:], hs[t][:], ACT.Sigmoid)
            result = sb([P, S], F32, "result%d" % t, tag=("excess3", "out_gate0", "out_gate1", None)[t])
            last = t == PACK - 1
            for cols in halves if last else [slice(0, S)]:
                (nc.vector if last else nc.gpsimd).tensor_tensor(result[:, cols], sents[t][:, cols], gate[:, cols], ALU.mult)
                (nc.scalar if last else nc.sync).dma_start(out=out_rows[:, t, cols], in_=result[:, cols])

        for stage in (fetch, send, finish):
            for t in range(PACK):
                stage(t)
